import numpy as np
import ml_dtypes


def mxq(x, axis, fmt="e4m3"):
    dtype, down = {"e4m3": (ml_dtypes.float8_e4m3fn, 7), "e5m2": (ml_dtypes.float8_e5m2, 14)}[fmt]
    v = np.moveaxis(np.asarray(x, np.float32).astype(ml_dtypes.bfloat16).astype(np.float64), axis, -1)
    blocks = v.reshape(v.shape[:-1] + (-1, 32))
    amax = np.abs(blocks).max(-1, keepdims=True)
    byte = np.maximum(np.where(amax > 0, np.frexp(amax)[1] - 1 + 127, 0) - down, 1)
    scale = np.exp2(byte - 127.0)
    codes = (blocks / scale).astype(np.float32).astype(dtype).astype(np.float64)
    return np.moveaxis((codes * scale).reshape(v.shape), -1, axis)


WIDE = False


def mx_kscale(k):
    if not WIDE:
        return np.ones(k)
    levels = np.array([10, -10, 5, -5, 0])
    if k % 512:
        return np.exp2(np.random.permutation(np.resize(levels, k // 32))).repeat(32)
    a = np.empty((k // 512, 16))
    for p in range(k // 512):
        a[p, :8] = np.random.permutation(np.resize(levels, 8))
        for g in range(8):
            far = levels[np.abs(levels - a[p, g]) >= 10]
            a[p, g + 8] = far[np.random.randint(len(far))]
    return np.exp2(a.ravel()).repeat(32)


def f64(x):
    return np.asarray(x).astype(np.float64)


def striped(idx):
    return np.tile(idx.reshape(-1, 16).T, (8, 1)).astype(np.uint16)


def unstriped(offs):
    return offs[:16].T.reshape(-1).astype(np.int64)


def striped8(idx):
    return np.concatenate([x.reshape(-1, 16).T for x in idx]).astype(np.uint16)


def runs(offs, k):
    lists = np.stack([offs[16 * r : 16 * r + 16].T.reshape(-1) for r in range(8)]).astype(np.int64)
    return lists[np.arange(k) % 512 // 64]


def pack_weight(w):
    k, n = w.shape
    w = f64(np.asarray(w, np.float32).astype(ml_dtypes.bfloat16)).reshape(k // 32, 32, n)
    amax = np.abs(w).max(1)
    byte = np.clip(np.where(amax > 0, np.frexp(amax)[1] - 1 + 127 - 7, 1), 1, 254)
    scaled = (w * np.exp2(127.0 - byte)[:, None, :]).reshape(k, n).astype(np.float32)
    words = np.ascontiguousarray(scaled.reshape(k // 512, 128, 4, n).transpose(0, 1, 3, 2)).astype(ml_dtypes.float8_e4m3fn).view(np.uint8)
    return words, np.ascontiguousarray(byte.astype(np.uint8).reshape(k // 512, 16, n))


def unpack_weight(words, scales):
    g, p, n, _ = words.shape
    vals = np.ascontiguousarray(words).view(ml_dtypes.float8_e4m3fn).astype(np.float64) * np.repeat(np.exp2(scales.astype(np.float64) - 127.0), 8, axis=1)[..., None]
    return vals.transpose(0, 1, 3, 2).reshape(g * 512, n)


def sigmoid(v):
    return 1.0 / (1.0 + np.exp(-np.maximum(v, -700.0)))


K, T, S, N, H, G, U = 512, 2048, 512, 512, 512, 2048, 1024


def setup_inputs():
    n = np.random.standard_normal
    s = mx_kscale(K)[:, None]
    u = mx_kscale(S)
    packed_xT = pack_weight(n((K, T)) * s)
    packed_dT = pack_weight(n((K, G)) / s)
    return {
        "x_words": packed_xT[0],
        "x_scales": packed_xT[1],
        "w1": (n((K, H)) / np.sqrt(K) / s).astype(np.float32),
        "d_words": packed_dT[0],
        "d_scales": packed_dT[1],
        "gn": (np.random.uniform(0.5, 1.5, (H, 1)) * u[:, None]).astype(np.float32),
        "w2": (n((H, N)) / np.sqrt(H) / u[:, None]).astype(np.float32),
        "mem": n((N, U)).astype(np.float32),
        "offs": striped(np.random.permutation(T)[:S]),
        "k1": striped8(np.random.randint(0, G, (8, H))),
        "two": striped(np.random.permutation(T)[:S]),
        "n1": striped8(np.stack([np.random.permutation(S) for _ in range(8)])),
        "n2": striped8(np.stack([np.random.permutation(S) for _ in range(8)])),
        "n3": striped8(np.stack([np.random.permutation(U)[:S] for _ in range(8)])),
    }


def reference(x_words, x_scales, w1, d_words, d_scales, gn, w2, mem, offs, k1, two, n1, n2, n3):
    old = f64(mem)[np.arange(N)[:, None], runs(n3, N)]
    xq = unpack_weight(x_words, x_scales)[:, unstriped(offs)]
    y = mxq(f64(w1), 0, "e4m3").T @ xq
    d_k1 = unpack_weight(d_words, d_scales)[np.arange(K)[:, None], runs(k1, K)]
    x_two = unpack_weight(x_words, x_scales)[:, unstriped(two)]
    d = 0.0625 * (d_k1.T @ x_two)
    z = f64(gn) * (y * (np.tanh(d[np.arange(H)[:, None], runs(n1, H)] - (d[np.arange(H)[:, None], runs(n2, H)]))))
    h = mxq(f64(w2), 0, "e4m3").T @ mxq(z, 0, "e4m3")
    nw = old + sigmoid(h) * (h - old)
    out = f64(mem).copy()
    out[np.arange(N)[:, None], runs(n3, N)] = nw
    return out

@@ -1,0 +1,205 @@
+from contextlib import ExitStack
+
+import concourse.mybir as mybir
+
+F32 = mybir.dt.float32
+BF16 = mybir.dt.bfloat16
+I32 = mybir.dt.int32
+U32 = mybir.dt.uint32
+U16 = mybir.dt.uint16
+U8 = mybir.dt.uint8
+FP8X4 = mybir.dt.float8_e4m3fn_x4
+ACT = mybir.ActivationFunctionType
+ALU = mybir.AluOpType
+
+P = 128
+PACK = 4
+K, T, S, N, H, G, U = 512, 2048, 512, 512, 512, 2048, 1024
+HALF = S // 2
+FLOPS = 3 * 2 * 512 * 512 * 512
+
+SLOT = {
+    "old00": "second03", "first10": "diff03", "second10": "th03",
+    "old01": "gate00", "kept01": "first10",
+    "first11": "old00", "second11": "kept00",
+    "kept02": "first11", "old02": "gate01",
+    "first12": "old01", "second12": "second10",
+    "first13": "second11", "second13": "diff10",
+    "old03": "second12",
+    "kept03": "z_rows1",
+    "old10": "diff13", "old11": "gate10", "old12": "gate11", "old13": "gate12",
+}
+
+
+def slot_of(name):
+    return slot_of(SLOT[name]) if name in SLOT else name
+
+
+def tile_picked_twkeyjointbpaget_none_p_kernel(tc, x_words, x_scales, w1, d_words, d_scales, gn, w2, mem, offs, k1, two, n1, n2, n3, out):
+    nc = tc.nc
+    with ExitStack() as ctx:
+        lists = ctx.enter_context(tc.tile_pool(name="lists", bufs=1))
+        keep = ctx.enter_context(tc.tile_pool(name="keep", bufs=1))
+        psum = ctx.enter_context(tc.psum_pool(name="psum", bufs=1))
+
+        def load_list(src, name):
+            tile = lists.tile([P, S // 16], U16, name=name)
+            nc.sync.dma_start(tile[:], src)
+            return tile
+
+        def dealt_rows(a, t):
+            return a.rearrange("(b t e) n -> t b e n", t=PACK, e=8)[t]
+
+        d_sc = keep.tile([P, G], U8, name="d_sc", align_bytes=64)
+        x_sc = keep.tile([P, T], U8, name="x_sc", align_bytes=64)
+        nc.vector.memset(d_sc[:].bitcast(I32), 0)
+        nc.vector.memset(x_sc[:].bitcast(I32), 0)
+
+        k1_l = load_list(k1, "k1_l")
+        two_l = load_list(two, "two_l")
+        offs_l = load_list(offs, "offs_l")
+        n1_l = load_list(n1, "n1_l")
+        n2_l = load_list(n2, "n2_l")
+        for e in range(2):
+            nc.sync.dma_start(d_sc[e:P:16, :].bitcast(I32), d_scales[0, e:16:2, :].bitcast(I32))
+        d_wd = keep.tile([P, G], U32, name="d_wd", align_bytes=64)
+        nc.sync.dma_start(d_wd[:].bitcast(I32), d_words[0].rearrange("p n r -> p (n r)").bitcast(I32))
+        for j in range(PACK):
+            nc.sync.dma_start(x_sc[j:P:32, :].bitcast(I32), x_scales[0, j:16:4, :].bitcast(I32))
+        x_wd = keep.tile([P, T], U32, name="x_wd", align_bytes=64)
+        nc.sync.dma_start(x_wd[:].bitcast(I32), x_words[0].rearrange("p n r -> p (n r)").bitcast(I32))
+        w1_raw = keep.tile([P, PACK, H], F32, name="w1_raw")
+        nc.sync.dma_start(w1_raw[:], w1.rearrange("(p j) c -> p j c", j=PACK))
+        n3_l = load_list(n3, "n3_l")
+        w2_raw = keep.tile([P, PACK, N], F32, name="w2_raw")
+        for t in range(PACK):
+            nc.sync.dma_start(w2_raw[:, t, :], dealt_rows(w2, t))
+        gain = []
+        for t in range(PACK):
+            tile = keep.tile([P, 1], F32, name="gain%d" % t)
+            with nc.allow_non_contiguous_dma(reason="one gain for each dealt row"):
+                nc.sync.dma_start(tile[:], dealt_rows(gn, t))
+            gain.append(tile)
+        page = []
+        for t in range(PACK):
+            tile = keep.tile([P, U], F32, name="page%d" % t)
+            nc.sync.dma_start(tile[:], dealt_rows(mem, t))
+            page.append(tile)
+
+        def gather(window, lst, dtype, name):
+            tile = keep.tile([P, S], dtype, name=name, align_bytes=64)
+            nc.vector.tensor_copy(tile[:], window[:].indirect(lst[:]))
+            return tile
+
+        def deal(src, dtype, view, run, name):
+            tile = keep.tile([P, S], dtype, name=name, align_bytes=64)
+            nc.vector.tensor_copy(
+                tile[:].bitcast(view).rearrange("p (t b e) -> p t b e", t=PACK, e=run),
+                src[:].bitcast(view).rearrange("p (b t e) -> p t b e", t=PACK, e=run),
+            )
+            return tile
+
+        dk_sc = gather(d_sc, k1_l, U8, "dk_sc")
+        dk_odd = deal(dk_sc, U8, I32, 2, "dk_odd")
+        dk_plane = deal(dk_sc, U8, I32, 2, "dk_plane")
+        for e in range(2):
+            nc.gpsimd.dma_start(dk_plane[2 + e : P : 32, :].bitcast(I32), dk_odd[16 + e : P : 32, :].bitcast(I32))
+        dk_wd = gather(d_wd, k1_l, U32, "dk_wd")
+        dk_codes = deal(dk_wd, U32, U32, 8, "dk_codes")
+        xt_sc = gather(x_sc, two_l, U8, "xt_sc")
+        xt_wd = gather(x_wd, two_l, U32, "xt_wd")
+
+        def product(acc, w_codes, w_plane, t, codes, plane):
+            cols = slice(t * P, (t + 1) * P)
+            nc.tensor.matmul_mx(out=acc, lhsT=w_codes[:, cols].bitcast(FP8X4), lhsT_scale=w_plane[:, cols],
+                                rhs=codes.bitcast(FP8X4), rhs_scale=plane, start=True, stop=True)
+
+        d_rows = []
+        for t in range(PACK):
+            acc = psum.tile([P, S], F32, name="d_acc", tag="bank%d" % t)
+            product(acc[:], dk_codes, dk_plane, t, xt_wd[:], xt_sc[:])
+            tile = keep.tile([P, S], F32, name="d_rows%d" % t)
+            nc.scalar.copy(tile[:], acc[:])
+            d_rows.append(tile)
+
+        xo_sc = gather(x_sc, offs_l, U8, "xo_sc")
+        xo_wd = gather(x_wd, offs_l, U32, "xo_wd")
+
+        def quantise_weight(raw, name):
+            rounded = keep.tile([P, PACK * H], BF16, name=name + "_bf", align_bytes=64)
+            nc.vector.tensor_copy(
+                rounded[:].rearrange("p (t b e j) -> p t b j e", t=PACK, e=8, j=PACK),
+                raw[:].rearrange("p j (b t e) -> p t b j e", t=PACK, e=8),
+            )
+            codes = keep.tile([P, H], U32, name=name + "_codes", align_bytes=64)
+            plane = keep.tile([P, H], U8, name=name + "_plane", align_bytes=64)
+            nc.vector.quantize_mx(out=codes[:].bitcast(FP8X4), scales=plane[:], in_=rounded[:])
+            return codes, plane
+
+        w1_codes, w1_plane = quantise_weight(w1_raw, "w1")
+        y_acc = []
+        for t in range(PACK):
+            acc = psum.tile([P, S], F32, name="y_acc", tag="bank%d" % (PACK + t))
+            product(acc[:], w1_codes, w1_plane, t, xo_wd[:], xo_sc[:])
+            y_acc.append(acc)
+
+        def piece(kind, hf, t):
+            name = "%s%d%d" % (kind, hf, t)
+            return keep.tile([P, HALF], F32, name=name, tag=slot_of(name))
+
+        def cols(hf):
+            return slice(hf * HALF, (hf + 1) * HALF)
+
+        def lcols(hf):
+            return slice(hf * HALF // 16, (hf + 1) * HALF // 16)
+
+        def z_row(hf, t, z_rows):
+            first = piece("first", hf, t)
+            nc.scalar.activation(first[:], d_rows[t][:].indirect(n1_l[:, lcols(hf)]), ACT.Copy)
+            second = piece("second", hf, t)
+            nc.scalar.activation(second[:], d_rows[t][:].indirect(n2_l[:, lcols(hf)]), ACT.Copy)
+            diff = piece("diff", hf, t)
+            nc.vector.tensor_tensor(diff[:], first[:], second[:], ALU.subtract)
+            th = piece("th", hf, t)
+            nc.scalar.activation(th[:], diff[:], ACT.Tanh, scale=0.0625)
+            nc.vector.scalar_tensor_tensor(z_rows[:, t, :], y_acc[t][:, cols(hf)], gain[t][:], th[:], ALU.mult, ALU.mult)
+
+        def quantise_z(hf, z_rows):
+            woven = keep.tile([P, PACK * HALF], BF16, name="woven%d" % hf, align_bytes=64)
+            nc.vector.tensor_copy(
+                woven[:].rearrange("p (c i t) -> p c t i", i=4, t=PACK),
+                z_rows[:].rearrange("p t (c i) -> p c t i", i=4),
+            )
+            codes = keep.tile([P, HALF], U32, name="z_codes%d" % hf, align_bytes=64)
+            plane = keep.tile([P, HALF], U8, name="z_plane%d" % hf, align_bytes=64)
+            nc.vector.quantize_mx(out=codes[:].bitcast(FP8X4), scales=plane[:], in_=woven[:])
+            return codes, plane
+
+        def write_page(hf, t, z):
+            old = piece("old", hf, t)
+            nc.scalar.activation(old[:], page[t][:].indirect(n3_l[:, lcols(hf)]), ACT.Copy, scale=-0.5)
+            acc = psum.tile([P, HALF], F32, name="h_acc", tag="bank%d" % t)
+            product(acc[:], w2_codes, w2_plane, t, z[0][:], z[1][:])
+            gate = piece("gate", hf, t)
+            nc.scalar.activation(gate[:], acc[:], ACT.Tanh, scale=0.5)
+            taken = piece("taken", hf, t)
+            nc.scalar.activation(taken[:], acc[:], ACT.Silu)
+            kept = piece("kept", hf, t)
+            nc.vector.scalar_tensor_tensor(kept[:], gate[:], 1.0, old[:], ALU.subtract, ALU.mult)
+            nc.vector.tensor_tensor(page[t][:].indirect(n3_l[:, lcols(hf)]), taken[:], kept[:], ALU.add)
+
+        rows0 = keep.tile([P, PACK, HALF], BF16, name="z_rows0", tag="z_rows0")
+        rows1 = keep.tile([P, PACK, HALF], BF16, name="z_rows1", tag="z_rows1")
+        for t in range(PACK):
+            z_row(0, t, rows0)
+        w2_codes, w2_plane = quantise_weight(w2_raw, "w2")
+        z0 = quantise_z(0, rows0)
+        for t in range(PACK - 1):
+            write_page(0, t, z0)
+            z_row(1, t, rows1)
+        z_row(1, PACK - 1, rows1)
+        z1 = quantise_z(1, rows1)
+        write_page(0, PACK - 1, z0)
+        for t in range(PACK):
+            write_page(1, t, z1)
+            nc.sync.dma_start(dealt_rows(out, t), page[t][:])

@@ -19,16 +19,23 @@ HALF = S // 2
 FLOPS = 3 * 2 * 512 * 512 * 512
 
 SLOT = {
-    "old00": "second03", "first10": "diff03", "second10": "th03",
-    "old01": "gate00", "kept01": "first10",
-    "first11": "old00", "second11": "kept00",
-    "kept02": "first11", "old02": "gate01",
-    "first12": "old01", "second12": "second10",
-    "first13": "second11", "second13": "diff10",
-    "old03": "second12",
-    "kept03": "z_rows1",
-    "old10": "diff13", "old11": "gate10", "old12": "gate11", "old13": "gate12",
+    "w1_raw": "dk_sc", "w2_raw": "dk_odd",
+    "gain0": "d_wd", "gain1": "dk_wd", "gain2": "xt_sc", "gain3": "dk_codes",
+    "page0": "x_sc", "page1": "x_wd", "page2": "w1_raw", "page3": "w2_raw",
+    "w2b_bf": "woven0",
+    "old00": "second03", "first12": "old00",
+    "first11": "first03", "gate02": "first11",
+    "first10": "diff03", "kept01": "first10",
+    "second10": "th03", "second12": "second10", "taken02": "second12",
+    "second11": "z_rows0",
+    "old01": "gate00", "first13": "old01", "old02": "first13",
+    "second13": "diff10", "old03": "second13",
+    "kept02": "th12",
+    "gate03": "diff13", "old10": "woven1", "old11": "gate03",
+    "taken03": "z_rows1",
+    "old12": "taken03", "old13": "gate10",
 }
+FUSED = ((0, 0), (0, 1))
 
 
 def slot_of(name):
@@ -47,52 +54,42 @@ def tile_picked_twkeyjointbpaget_none_p_kernel(tc, x_words, x_scales, w1, d_word
             nc.sync.dma_start(tile[:], src)
             return tile
 
+        def held(shape, dtype, name):
+            return keep.tile(shape, dtype, name=name, tag=slot_of(name), align_bytes=64)
+
         def dealt_rows(a, t):
             return a.rearrange("(b t e) n -> t b e n", t=PACK, e=8)[t]
 
-        d_sc = keep.tile([P, G], U8, name="d_sc", align_bytes=64)
-        x_sc = keep.tile([P, T], U8, name="x_sc", align_bytes=64)
-        nc.vector.memset(d_sc[:].bitcast(I32), 0)
+        d_sc = held([P, G], U8, "d_sc")
+        x_sc = held([P, T], U8, "x_sc")
+        nc.gpsimd.memset(d_sc[:].bitcast(I32), 0)
         nc.vector.memset(x_sc[:].bitcast(I32), 0)
 
+        warm = held([P, 8], F32, "warm")
+        nc.gpsimd.memset(warm[:], 0.0)
+        nc.scalar.activation(warm[:, 0:1], warm[:, 4:5], ACT.Silu)
         k1_l = load_list(k1, "k1_l")
         two_l = load_list(two, "two_l")
-        offs_l = load_list(offs, "offs_l")
         n1_l = load_list(n1, "n1_l")
         n2_l = load_list(n2, "n2_l")
         for e in range(2):
             nc.sync.dma_start(d_sc[e:P:16, :].bitcast(I32), d_scales[0, e:16:2, :].bitcast(I32))
-        d_wd = keep.tile([P, G], U32, name="d_wd", align_bytes=64)
+        d_wd = held([P, G], U32, "d_wd")
         nc.sync.dma_start(d_wd[:].bitcast(I32), d_words[0].rearrange("p n r -> p (n r)").bitcast(I32))
         for j in range(PACK):
             nc.sync.dma_start(x_sc[j:P:32, :].bitcast(I32), x_scales[0, j:16:4, :].bitcast(I32))
-        x_wd = keep.tile([P, T], U32, name="x_wd", align_bytes=64)
+        x_wd = held([P, T], U32, "x_wd")
         nc.sync.dma_start(x_wd[:].bitcast(I32), x_words[0].rearrange("p n r -> p (n r)").bitcast(I32))
-        w1_raw = keep.tile([P, PACK, H], F32, name="w1_raw")
-        nc.sync.dma_start(w1_raw[:], w1.rearrange("(p j) c -> p j c", j=PACK))
+        offs_l = load_list(offs, "offs_l")
         n3_l = load_list(n3, "n3_l")
-        w2_raw = keep.tile([P, PACK, N], F32, name="w2_raw")
-        for t in range(PACK):
-            nc.sync.dma_start(w2_raw[:, t, :], dealt_rows(w2, t))
-        gain = []
-        for t in range(PACK):
-            tile = keep.tile([P, 1], F32, name="gain%d" % t)
-            with nc.allow_non_contiguous_dma(reason="one gain for each dealt row"):
-                nc.sync.dma_start(tile[:], dealt_rows(gn, t))
-            gain.append(tile)
-        page = []
-        for t in range(PACK):
-            tile = keep.tile([P, U], F32, name="page%d" % t)
-            nc.sync.dma_start(tile[:], dealt_rows(mem, t))
-            page.append(tile)
 
         def gather(window, lst, dtype, name):
-            tile = keep.tile([P, S], dtype, name=name, align_bytes=64)
+            tile = held([P, S], dtype, name)
             nc.vector.tensor_copy(tile[:], window[:].indirect(lst[:]))
             return tile
 
         def deal(src, dtype, view, run, name):
-            tile = keep.tile([P, S], dtype, name=name, align_bytes=64)
+            tile = held([P, S], dtype, name)
             nc.vector.tensor_copy(
                 tile[:].bitcast(view).rearrange("p (t b e) -> p t b e", t=PACK, e=run),
                 src[:].bitcast(view).rearrange("p (b t e) -> p t b e", t=PACK, e=run),
@@ -103,7 +100,12 @@ def tile_picked_twkeyjointbpaget_none_p_kernel(tc, x_words, x_scales, w1, d_word
         dk_odd = deal(dk_sc, U8, I32, 2, "dk_odd")
         dk_plane = deal(dk_sc, U8, I32, 2, "dk_plane")
         for e in range(2):
-            nc.gpsimd.dma_start(dk_plane[2 + e : P : 32, :].bitcast(I32), dk_odd[16 + e : P : 32, :].bitcast(I32))
+            nc.sync.dma_start(dk_plane[2 + e : P : 32, :].bitcast(I32), dk_odd[16 + e : P : 32, :].bitcast(I32))
+        w1_raw = held([P, PACK, H], F32, "w1_raw")
+        nc.sync.dma_start(w1_raw[:], w1.rearrange("(p j) c -> p j c", j=PACK))
+        w2_raw = held([P, PACK, N], F32, "w2_raw")
+        for t in range(PACK):
+            nc.sync.dma_start(w2_raw[:, t, :], dealt_rows(w2, t))
         dk_wd = gather(d_wd, k1_l, U32, "dk_wd")
         dk_codes = deal(dk_wd, U32, U32, 8, "dk_codes")
         xt_sc = gather(x_sc, two_l, U8, "xt_sc")
@@ -118,34 +120,46 @@ def tile_picked_twkeyjointbpaget_none_p_kernel(tc, x_words, x_scales, w1, d_word
         for t in range(PACK):
             acc = psum.tile([P, S], F32, name="d_acc", tag="bank%d" % t)
             product(acc[:], dk_codes, dk_plane, t, xt_wd[:], xt_sc[:])
-            tile = keep.tile([P, S], F32, name="d_rows%d" % t)
+            tile = held([P, S], F32, "d_rows%d" % t)
             nc.scalar.copy(tile[:], acc[:])
             d_rows.append(tile)
 
+        gain = []
+        for t in range(PACK):
+            tile = held([P, 1], F32, "gain%d" % t)
+            with nc.allow_non_contiguous_dma(reason="one gain for each dealt row"):
+                nc.sync.dma_start(tile[:], dealt_rows(gn, t))
+            gain.append(tile)
         xo_sc = gather(x_sc, offs_l, U8, "xo_sc")
         xo_wd = gather(x_wd, offs_l, U32, "xo_wd")
 
-        def quantise_weight(raw, name):
-            rounded = keep.tile([P, PACK * H], BF16, name=name + "_bf", align_bytes=64)
+        def quantise_weight(raw, t0, t1, name):
+            width = (t1 - t0) * P
+            rounded = held([P, PACK * width], BF16, name + "_bf")
             nc.vector.tensor_copy(
-                rounded[:].rearrange("p (t b e j) -> p t b j e", t=PACK, e=8, j=PACK),
-                raw[:].rearrange("p j (b t e) -> p t b j e", t=PACK, e=8),
+                rounded[:].rearrange("p (t b e j) -> p t b j e", b=16, e=8, j=PACK),
+                raw[:].rearrange("p j (b t e) -> p t b j e", t=PACK, e=8)[:, t0:t1],
             )
-            codes = keep.tile([P, H], U32, name=name + "_codes", align_bytes=64)
-            plane = keep.tile([P, H], U8, name=name + "_plane", align_bytes=64)
+            codes = held([P, width], U32, name + "_codes")
+            plane = held([P, width], U8, name + "_plane")
             nc.vector.quantize_mx(out=codes[:].bitcast(FP8X4), scales=plane[:], in_=rounded[:])
             return codes, plane
 
-        w1_codes, w1_plane = quantise_weight(w1_raw, "w1")
-        y_acc = []
-        for t in range(PACK):
-            acc = psum.tile([P, S], F32, name="y_acc", tag="bank%d" % (PACK + t))
-            product(acc[:], w1_codes, w1_plane, t, xo_wd[:], xo_sc[:])
-            y_acc.append(acc)
+        w1_codes, w1_plane = quantise_weight(w1_raw, 0, PACK, "w1")
+
+        page = []
+
+        def load_page(t):
+            tile = held([P, U], F32, "page%d" % t)
+            nc.sync.dma_start(tile[:], dealt_rows(mem, t))
+            page.append(tile)
+
+        for t in range(PACK - 1):
+            load_page(t)
 
         def piece(kind, hf, t):
             name = "%s%d%d" % (kind, hf, t)
-            return keep.tile([P, HALF], F32, name=name, tag=slot_of(name))
+            return held([P, HALF], F32, name)
 
         def cols(hf):
             return slice(hf * HALF, (hf + 1) * HALF)
@@ -156,50 +170,72 @@ def tile_picked_twkeyjointbpaget_none_p_kernel(tc, x_words, x_scales, w1, d_word
         def z_row(hf, t, z_rows):
             first = piece("first", hf, t)
             nc.scalar.activation(first[:], d_rows[t][:].indirect(n1_l[:, lcols(hf)]), ACT.Copy)
-            second = piece("second", hf, t)
-            nc.scalar.activation(second[:], d_rows[t][:].indirect(n2_l[:, lcols(hf)]), ACT.Copy)
             diff = piece("diff", hf, t)
-            nc.vector.tensor_tensor(diff[:], first[:], second[:], ALU.subtract)
+            if (hf, t) in FUSED:
+                nc.vector.tensor_tensor(diff[:], d_rows[t][:].indirect(n2_l[:, lcols(hf)]), first[:], ALU.subtract)
+            else:
+                second = piece("second", hf, t)
+                nc.scalar.activation(second[:], d_rows[t][:].indirect(n2_l[:, lcols(hf)]), ACT.Copy)
+                nc.vector.tensor_tensor(diff[:], second[:], first[:], ALU.subtract)
             th = piece("th", hf, t)
-            nc.scalar.activation(th[:], diff[:], ACT.Tanh, scale=0.0625)
-            nc.vector.scalar_tensor_tensor(z_rows[:, t, :], y_acc[t][:, cols(hf)], gain[t][:], th[:], ALU.mult, ALU.mult)
+            nc.scalar.activation(th[:], diff[:], ACT.Tanh, scale=-0.0625)
+            y_acc = psum.tile([P, HALF], F32, name="y_acc", tag="bank%d" % (PACK + t))
+            product(y_acc[:], w1_codes, w1_plane, t, xo_wd[:, cols(hf)], xo_sc[:, cols(hf)])
+            nc.vector.scalar_tensor_tensor(z_rows[:, t, :], y_acc[:], gain[t][:], th[:], ALU.mult, ALU.mult)
 
         def quantise_z(hf, z_rows):
-            woven = keep.tile([P, PACK * HALF], BF16, name="woven%d" % hf, align_bytes=64)
-            nc.vector.tensor_copy(
+            woven = held([P, PACK * HALF], BF16, "woven%d" % hf)
+            weave = nc.vector.tensor_copy if hf == 0 else nc.scalar.copy
+            weave(
                 woven[:].rearrange("p (c i t) -> p c t i", i=4, t=PACK),
                 z_rows[:].rearrange("p t (c i) -> p c t i", i=4),
             )
-            codes = keep.tile([P, HALF], U32, name="z_codes%d" % hf, align_bytes=64)
-            plane = keep.tile([P, HALF], U8, name="z_plane%d" % hf, align_bytes=64)
+            codes = held([P, HALF], U32, "z_codes%d" % hf)
+            plane = held([P, HALF], U8, "z_plane%d" % hf)
             nc.vector.quantize_mx(out=codes[:].bitcast(FP8X4), scales=plane[:], in_=woven[:])
             return codes, plane
 
-        def write_page(hf, t, z):
+        def keep_part(hf, t, z):
             old = piece("old", hf, t)
             nc.scalar.activation(old[:], page[t][:].indirect(n3_l[:, lcols(hf)]), ACT.Copy, scale=-0.5)
             acc = psum.tile([P, HALF], F32, name="h_acc", tag="bank%d" % t)
-            product(acc[:], w2_codes, w2_plane, t, z[0][:], z[1][:])
+            w2_q, at = (w2_first, 0) if t == 0 else (w2_rest, t - 1)
+            product(acc[:], w2_q[0], w2_q[1], at, z[0][:], z[1][:])
             gate = piece("gate", hf, t)
             nc.scalar.activation(gate[:], acc[:], ACT.Tanh, scale=0.5)
-            taken = piece("taken", hf, t)
-            nc.scalar.activation(taken[:], acc[:], ACT.Silu)
             kept = piece("kept", hf, t)
             nc.vector.scalar_tensor_tensor(kept[:], gate[:], 1.0, old[:], ALU.subtract, ALU.mult)
+            return acc, kept
+
+        def put_part(hf, t, part):
+            acc, kept = part
+            taken = piece("taken", hf, t)
+            nc.scalar.activation(taken[:], acc[:], ACT.Silu)
             nc.vector.tensor_tensor(page[t][:].indirect(n3_l[:, lcols(hf)]), taken[:], kept[:], ALU.add)
 
-        rows0 = keep.tile([P, PACK, HALF], BF16, name="z_rows0", tag="z_rows0")
-        rows1 = keep.tile([P, PACK, HALF], BF16, name="z_rows1", tag="z_rows1")
+        rows0 = held([P, PACK, HALF], BF16, "z_rows0")
+        rows1 = held([P, PACK, HALF], BF16, "z_rows1")
         for t in range(PACK):
             z_row(0, t, rows0)
-        w2_codes, w2_plane = quantise_weight(w2_raw, "w2")
+        w2_first = quantise_weight(w2_raw, 0, 1, "w2a")
         z0 = quantise_z(0, rows0)
-        for t in range(PACK - 1):
-            write_page(0, t, z0)
-            z_row(1, t, rows1)
-        z_row(1, PACK - 1, rows1)
+        w2_rest = quantise_weight(w2_raw, 1, PACK, "w2b")
+        load_page(PACK - 1)
+        put_part(0, 0, keep_part(0, 0, z0))
+        z_row(1, 0, rows1)
+        part = keep_part(0, 1, z0)
+        z_row(1, 1, rows1)
+        put_part(0, 1, part)
+        z_row(1, 2, rows1)
+        z_row(1, 3, rows1)
+        part = keep_part(0, 2, z0)
+        last = keep_part(0, 3, z0)
+        put_part(0, 2, part)
         z1 = quantise_z(1, rows1)
-        write_page(0, PACK - 1, z0)
+        put_part(0, 3, last)
+        parts = [keep_part(1, 0, z1)]
         for t in range(PACK):
-            write_page(1, t, z1)
+            if t + 1 < PACK:
+                parts.append(keep_part(1, t + 1, z1))
+            put_part(1, t, parts[t])
             nc.sync.dma_start(dealt_rows(out, t), page[t][:])

@@ -19,23 +19,18 @@ HALF = S // 2
 FLOPS = 3 * 2 * 512 * 512 * 512
 
 SLOT = {
-    "w1_raw": "dk_sc", "w2_raw": "dk_odd",
-    "gain0": "d_wd", "gain1": "dk_wd", "gain2": "xt_sc", "gain3": "dk_codes",
+    "w1_raw": "dk_sc", "w2_raw": "dk_wd",
     "page0": "x_sc", "page1": "x_wd", "page2": "w1_raw", "page3": "w2_raw",
-    "w2b_bf": "woven0",
-    "old00": "second03", "first12": "old00",
-    "first11": "first03", "gate02": "first11",
-    "first10": "diff03", "kept01": "first10",
-    "second10": "th03", "second12": "second10", "taken02": "second12",
-    "second11": "z_rows0",
-    "old01": "gate00", "first13": "old01", "old02": "first13",
-    "second13": "diff10", "old03": "second13",
-    "kept02": "th12",
-    "gate03": "diff13", "old10": "woven1", "old11": "gate03",
-    "taken03": "z_rows1",
-    "old12": "taken03", "old13": "gate10",
+    "first10": "diff03", "first11": "first03",
+    "old00": "th02", "first12": "old00", "kept01": "first12",
+    "w2b_bf": "th03",
+    "first13": "gate00", "old02": "first13",
+    "old01": "kept00",
+    "gate02": "diff12", "taken02": "th11", "kept02": "th12",
+    "old03": "gate01", "gate03": "diff13", "taken03": "z_rows1",
+    "old10": "woven1", "old11": "gate03", "old12": "taken03", "old13": "gate10",
 }
-FUSED = ((0, 0), (0, 1))
+FUSED = tuple((hf, t) for hf in range(2) for t in range(4))
 
 
 def slot_of(name):
@@ -103,11 +98,11 @@ def tile_picked_twkeyjointbpaget_none_p_kernel(tc, x_words, x_scales, w1, d_word
             nc.sync.dma_start(dk_plane[2 + e : P : 32, :].bitcast(I32), dk_odd[16 + e : P : 32, :].bitcast(I32))
         w1_raw = held([P, PACK, H], F32, "w1_raw")
         nc.sync.dma_start(w1_raw[:], w1.rearrange("(p j) c -> p j c", j=PACK))
+        dk_wd = gather(d_wd, k1_l, U32, "dk_wd")
+        dk_codes = deal(dk_wd, U32, U32, 8, "dk_codes")
         w2_raw = held([P, PACK, N], F32, "w2_raw")
         for t in range(PACK):
             nc.sync.dma_start(w2_raw[:, t, :], dealt_rows(w2, t))
-        dk_wd = gather(d_wd, k1_l, U32, "dk_wd")
-        dk_codes = deal(dk_wd, U32, U32, 8, "dk_codes")
         xt_sc = gather(x_sc, two_l, U8, "xt_sc")
         xt_wd = gather(x_wd, two_l, U32, "xt_wd")
 
@@ -128,24 +123,27 @@ def tile_picked_twkeyjointbpaget_none_p_kernel(tc, x_words, x_scales, w1, d_word
         for t in range(PACK):
             tile = held([P, 1], F32, "gain%d" % t)
             with nc.allow_non_contiguous_dma(reason="one gain for each dealt row"):
-                nc.sync.dma_start(tile[:], dealt_rows(gn, t))
+                nc.gpsimd.dma_start(tile[:], dealt_rows(gn, t))
             gain.append(tile)
         xo_sc = gather(x_sc, offs_l, U8, "xo_sc")
         xo_wd = gather(x_wd, offs_l, U32, "xo_wd")
 
-        def quantise_weight(raw, t0, t1, name):
+        def quantise_weight(raw, t0, t1, name, on_scalar):
             width = (t1 - t0) * P
             rounded = held([P, PACK * width], BF16, name + "_bf")
-            nc.vector.tensor_copy(
-                rounded[:].rearrange("p (t b e j) -> p t b j e", b=16, e=8, j=PACK),
-                raw[:].rearrange("p j (b t e) -> p t b j e", t=PACK, e=8)[:, t0:t1],
-            )
+            dst = rounded[:].rearrange("p (t b e j) -> p b t j e", b=16, e=8, j=PACK)
+            src = raw[:].rearrange("p j (b t e) -> p b t j e", t=PACK, e=8)
+            if on_scalar:
+                for t in range(t0, t1):
+                    nc.scalar.copy(dst[:, :, t - t0], src[:, :, t])
+            else:
+                nc.vector.tensor_copy(dst, src[:, :, t0:t1])
             codes = held([P, width], U32, name + "_codes")
             plane = held([P, width], U8, name + "_plane")
             nc.vector.quantize_mx(out=codes[:].bitcast(FP8X4), scales=plane[:], in_=rounded[:])
             return codes, plane
 
-        w1_codes, w1_plane = quantise_weight(w1_raw, 0, PACK, "w1")
+        w1_q = [quantise_weight(w1_raw, 0, 2, "w1a", True), quantise_weight(w1_raw, 2, PACK, "w1b", False)]
 
         page = []
 
@@ -180,13 +178,12 @@ def tile_picked_twkeyjointbpaget_none_p_kernel(tc, x_words, x_scales, w1, d_word
             th = piece("th", hf, t)
             nc.scalar.activation(th[:], diff[:], ACT.Tanh, scale=-0.0625)
             y_acc = psum.tile([P, HALF], F32, name="y_acc", tag="bank%d" % (PACK + t))
-            product(y_acc[:], w1_codes, w1_plane, t, xo_wd[:, cols(hf)], xo_sc[:, cols(hf)])
+            product(y_acc[:], w1_q[t // 2][0], w1_q[t // 2][1], t % 2, xo_wd[:, cols(hf)], xo_sc[:, cols(hf)])
             nc.vector.scalar_tensor_tensor(z_rows[:, t, :], y_acc[:], gain[t][:], th[:], ALU.mult, ALU.mult)
 
         def quantise_z(hf, z_rows):
             woven = held([P, PACK * HALF], BF16, "woven%d" % hf)
-            weave = nc.vector.tensor_copy if hf == 0 else nc.scalar.copy
-            weave(
+            nc.vector.tensor_copy(
                 woven[:].rearrange("p (c i t) -> p c t i", i=4, t=PACK),
                 z_rows[:].rearrange("p t (c i) -> p c t i", i=4),
             )
@@ -217,17 +214,17 @@ def tile_picked_twkeyjointbpaget_none_p_kernel(tc, x_words, x_scales, w1, d_word
         rows1 = held([P, PACK, HALF], BF16, "z_rows1")
         for t in range(PACK):
             z_row(0, t, rows0)
-        w2_first = quantise_weight(w2_raw, 0, 1, "w2a")
+        w2_first = quantise_weight(w2_raw, 0, 1, "w2a", False)
         z0 = quantise_z(0, rows0)
-        w2_rest = quantise_weight(w2_raw, 1, PACK, "w2b")
-        load_page(PACK - 1)
         put_part(0, 0, keep_part(0, 0, z0))
         z_row(1, 0, rows1)
-        part = keep_part(0, 1, z0)
         z_row(1, 1, rows1)
-        put_part(0, 1, part)
+        w2_rest = quantise_weight(w2_raw, 1, PACK, "w2b", True)
+        load_page(PACK - 1)
         z_row(1, 2, rows1)
+        part = keep_part(0, 1, z0)
         z_row(1, 3, rows1)
+        put_part(0, 1, part)
         part = keep_part(0, 2, z0)
         last = keep_part(0, 3, z0)
         put_part(0, 2, part)

from contextlib import ExitStack

import concourse.mybir as mybir

F32 = mybir.dt.float32
BF16 = mybir.dt.bfloat16
I32 = mybir.dt.int32
U32 = mybir.dt.uint32
U16 = mybir.dt.uint16
U8 = mybir.dt.uint8
FP8X4 = mybir.dt.float8_e4m3fn_x4
ACT = mybir.ActivationFunctionType
ALU = mybir.AluOpType

P = 128
PACK = 4
K, T, S, N, H, G, U = 512, 2048, 512, 512, 512, 2048, 1024
HALF = S // 2
FLOPS = 3 * 2 * 512 * 512 * 512

SLOT = {
    "w1_raw": "dk_sc", "w2_raw": "dk_wd",
    "page0": "x_sc", "page1": "x_wd", "page2": "w1_raw", "page3": "w2_raw",
    "first10": "diff03", "first11": "first03",
    "old00": "th02", "first12": "old00", "kept01": "first12",
    "w2b_bf": "th03",
    "first13": "gate00", "old02": "first13",
    "old01": "kept00",
    "gate02": "diff12", "taken02": "th11", "kept02": "th12",
    "old03": "gate01", "gate03": "diff13", "taken03": "z_rows1",
    "old10": "woven1", "old11": "gate03", "old12": "taken03", "old13": "gate10",
}
FUSED = tuple((hf, t) for hf in range(2) for t in range(4))


def slot_of(name):
    return slot_of(SLOT[name]) if name in SLOT else name


def tile_picked_twkeyjointbpaget_none_p_kernel(tc, x_words, x_scales, w1, d_words, d_scales, gn, w2, mem, offs, k1, two, n1, n2, n3, out):
    nc = tc.nc
    with ExitStack() as ctx:
        lists = ctx.enter_context(tc.tile_pool(name="lists", bufs=1))
        keep = ctx.enter_context(tc.tile_pool(name="keep", bufs=1))
        psum = ctx.enter_context(tc.psum_pool(name="psum", bufs=1))

        def load_list(src, name):
            tile = lists.tile([P, S // 16], U16, name=name)
            nc.sync.dma_start(tile[:], src)
            return tile

        def held(shape, dtype, name):
            return keep.tile(shape, dtype, name=name, tag=slot_of(name), align_bytes=64)

        def dealt_rows(a, t):
            return a.rearrange("(b t e) n -> t b e n", t=PACK, e=8)[t]

        d_sc = held([P, G], U8, "d_sc")
        x_sc = held([P, T], U8, "x_sc")
        nc.gpsimd.memset(d_sc[:].bitcast(I32), 0)
        nc.vector.memset(x_sc[:].bitcast(I32), 0)

        warm = held([P, 8], F32, "warm")
        nc.gpsimd.memset(warm[:], 0.0)
        nc.scalar.activation(warm[:, 0:1], warm[:, 4:5], ACT.Silu)
        k1_l = load_list(k1, "k1_l")
        two_l = load_list(two, "two_l")
        n1_l = load_list(n1, "n1_l")
        n2_l = load_list(n2, "n2_l")
        for e in range(2):
            nc.sync.dma_start(d_sc[e:P:16, :].bitcast(I32), d_scales[0, e:16:2, :].bitcast(I32))
        d_wd = held([P, G], U32, "d_wd")
        nc.sync.dma_start(d_wd[:].bitcast(I32), d_words[0].rearrange("p n r -> p (n r)").bitcast(I32))
        for j in range(PACK):
            nc.sync.dma_start(x_sc[j:P:32, :].bitcast(I32), x_scales[0, j:16:4, :].bitcast(I32))
        x_wd = held([P, T], U32, "x_wd")
        nc.sync.dma_start(x_wd[:].bitcast(I32), x_words[0].rearrange("p n r -> p (n r)").bitcast(I32))
        offs_l = load_list(offs, "offs_l")
        n3_l = load_list(n3, "n3_l")

        def gather(window, lst, dtype, name):
            tile = held([P, S], dtype, name)
            nc.vector.tensor_copy(tile[:], window[:].indirect(lst[:]))
            return tile

        def deal(src, dtype, view, run, name):
            tile = held([P, S], dtype, name)
            nc.vector.tensor_copy(
                tile[:].bitcast(view).rearrange("p (t b e) -> p t b e", t=PACK, e=run),
                src[:].bitcast(view).rearrange("p (b t e) -> p t b e", t=PACK, e=run),
            )
            return tile

        dk_sc = gather(d_sc, k1_l, U8, "dk_sc")
        dk_odd = deal(dk_sc, U8, I32, 2, "dk_odd")
        dk_plane = deal(dk_sc, U8, I32, 2, "dk_plane")
        for e in range(2):
            nc.sync.dma_start(dk_plane[2 + e : P : 32, :].bitcast(I32), dk_odd[16 + e : P : 32, :].bitcast(I32))
        w1_raw = held([P, PACK, H], F32, "w1_raw")
        nc.sync.dma_start(w1_raw[:], w1.rearrange("(p j) c -> p j c", j=PACK))
        dk_wd = gather(d_wd, k1_l, U32, "dk_wd")
        dk_codes = deal(dk_wd, U32, U32, 8, "dk_codes")
        w2_raw = held([P, PACK, N], F32, "w2_raw")
        for t in range(PACK):
            nc.sync.dma_start(w2_raw[:, t, :], dealt_rows(w2, t))
        xt_sc = gather(x_sc, two_l, U8, "xt_sc")
        xt_wd = gather(x_wd, two_l, U32, "xt_wd")

        def product(acc, w_codes, w_plane, t, codes, plane):
            cols = slice(t * P, (t + 1) * P)
            nc.tensor.matmul_mx(out=acc, lhsT=w_codes[:, cols].bitcast(FP8X4), lhsT_scale=w_plane[:, cols],
                                rhs=codes.bitcast(FP8X4), rhs_scale=plane, start=True, stop=True)

        d_rows = []
        for t in range(PACK):
            acc = psum.tile([P, S], F32, name="d_acc", tag="bank%d" % t)
            product(acc[:], dk_codes, dk_plane, t, xt_wd[:], xt_sc[:])
            tile = held([P, S], F32, "d_rows%d" % t)
            nc.scalar.copy(tile[:], acc[:])
            d_rows.append(tile)

        gain = []
        for t in range(PACK):
            tile = held([P, 1], F32, "gain%d" % t)
            with nc.allow_non_contiguous_dma(reason="one gain for each dealt row"):
                nc.gpsimd.dma_start(tile[:], dealt_rows(gn, t))
            gain.append(tile)
        xo_sc = gather(x_sc, offs_l, U8, "xo_sc")
        xo_wd = gather(x_wd, offs_l, U32, "xo_wd")

        def quantise_weight(raw, t0, t1, name, on_scalar):
            width = (t1 - t0) * P
            rounded = held([P, PACK * width], BF16, name + "_bf")
            dst = rounded[:].rearrange("p (t b e j) -> p b t j e", b=16, e=8, j=PACK)
            src = raw[:].rearrange("p j (b t e) -> p b t j e", t=PACK, e=8)
            if on_scalar:
                for t in range(t0, t1):
                    nc.scalar.copy(dst[:, :, t - t0], src[:, :, t])
            else:
                nc.vector.tensor_copy(dst, src[:, :, t0:t1])
            codes = held([P, width], U32, name + "_codes")
            plane = held([P, width], U8, name + "_plane")
            nc.vector.quantize_mx(out=codes[:].bitcast(FP8X4), scales=plane[:], in_=rounded[:])
            return codes, plane

        w1_q = [quantise_weight(w1_raw, 0, 2, "w1a", True), quantise_weight(w1_raw, 2, PACK, "w1b", False)]

        page = []

        def load_page(t):
            tile = held([P, U], F32, "page%d" % t)
            nc.sync.dma_start(tile[:], dealt_rows(mem, t))
            page.append(tile)

        for t in range(PACK - 1):
            load_page(t)

        def piece(kind, hf, t):
            name = "%s%d%d" % (kind, hf, t)
            return held([P, HALF], F32, name)

        def cols(hf):
            return slice(hf * HALF, (hf + 1) * HALF)

        def lcols(hf):
            return slice(hf * HALF // 16, (hf + 1) * HALF // 16)

        def z_row(hf, t, z_rows):
            first = piece("first", hf, t)
            nc.scalar.activation(first[:], d_rows[t][:].indirect(n1_l[:, lcols(hf)]), ACT.Copy)
            diff = piece("diff", hf, t)
            if (hf, t) in FUSED:
                nc.vector.tensor_tensor(diff[:], d_rows[t][:].indirect(n2_l[:, lcols(hf)]), first[:], ALU.subtract)
            else:
                second = piece("second", hf, t)
                nc.scalar.activation(second[:], d_rows[t][:].indirect(n2_l[:, lcols(hf)]), ACT.Copy)
                nc.vector.tensor_tensor(diff[:], second[:], first[:], ALU.subtract)
            th = piece("th", hf, t)
            nc.scalar.activation(th[:], diff[:], ACT.Tanh, scale=-0.0625)
            y_acc = psum.tile([P, HALF], F32, name="y_acc", tag="bank%d" % (PACK + t))
            product(y_acc[:], w1_q[t // 2][0], w1_q[t // 2][1], t % 2, xo_wd[:, cols(hf)], xo_sc[:, cols(hf)])
            nc.vector.scalar_tensor_tensor(z_rows[:, t, :], y_acc[:], gain[t][:], th[:], ALU.mult, ALU.mult)

        def quantise_z(hf, z_rows):
            woven = held([P, PACK * HALF], BF16, "woven%d" % hf)
            nc.vector.tensor_copy(
                woven[:].rearrange("p (c i t) -> p c t i", i=4, t=PACK),
                z_rows[:].rearrange("p t (c i) -> p c t i", i=4),
            )
            codes = held([P, HALF], U32, "z_codes%d" % hf)
            plane = held([P, HALF], U8, "z_plane%d" % hf)
            nc.vector.quantize_mx(out=codes[:].bitcast(FP8X4), scales=plane[:], in_=woven[:])
            return codes, plane

        def keep_part(hf, t, z):
            old = piece("old", hf, t)
            nc.scalar.activation(old[:], page[t][:].indirect(n3_l[:, lcols(hf)]), ACT.Copy, scale=-0.5)
            acc = psum.tile([P, HALF], F32, name="h_acc", tag="bank%d" % t)
            w2_q, at = (w2_first, 0) if t == 0 else (w2_rest, t - 1)
            product(acc[:], w2_q[0], w2_q[1], at, z[0][:], z[1][:])
            gate = piece("gate", hf, t)
            nc.scalar.activation(gate[:], acc[:], ACT.Tanh, scale=0.5)
            kept = piece("kept", hf, t)
            nc.vector.scalar_tensor_tensor(kept[:], gate[:], 1.0, old[:], ALU.subtract, ALU.mult)
            return acc, kept

        def put_part(hf, t, part):
            acc, kept = part
            taken = piece("taken", hf, t)
            nc.scalar.activation(taken[:], acc[:], ACT.Silu)
            nc.vector.tensor_tensor(page[t][:].indirect(n3_l[:, lcols(hf)]), taken[:], kept[:], ALU.add)

        rows0 = held([P, PACK, HALF], BF16, "z_rows0")
        rows1 = held([P, PACK, HALF], BF16, "z_rows1")
        for t in range(PACK):
            z_row(0, t, rows0)
        w2_first = quantise_weight(w2_raw, 0, 1, "w2a", False)
        z0 = quantise_z(0, rows0)
        put_part(0, 0, keep_part(0, 0, z0))
        z_row(1, 0, rows1)
        z_row(1, 1, rows1)
        w2_rest = quantise_weight(w2_raw, 1, PACK, "w2b", True)
        load_page(PACK - 1)
        z_row(1, 2, rows1)
        part = keep_part(0, 1, z0)
        z_row(1, 3, rows1)
        put_part(0, 1, part)
        part = keep_part(0, 2, z0)
        last = keep_part(0, 3, z0)
        put_part(0, 2, part)
        z1 = quantise_z(1, rows1)
        put_part(0, 3, last)
        parts = [keep_part(1, 0, z1)]
        for t in range(PACK):
            if t + 1 < PACK:
                parts.append(keep_part(1, t + 1, z1))
            put_part(1, t, parts[t])
            nc.sync.dma_start(dealt_rows(out, t), page[t][:])
